import numpy as np
import ml_dtypes


def mxq(x, axis, fmt="e4m3"):
    dtype, down = {"e4m3": (ml_dtypes.float8_e4m3fn, 7), "e5m2": (ml_dtypes.float8_e5m2, 14)}[fmt]
    v = np.moveaxis(np.asarray(x, np.float32).astype(ml_dtypes.bfloat16).astype(np.float64), axis, -1)
    blocks = v.reshape(v.shape[:-1] + (-1, 32))
    amax = np.abs(blocks).max(-1, keepdims=True)
    byte = np.maximum(np.where(amax > 0, np.frexp(amax)[1] - 1 + 127, 0) - down, 1)
    scale = np.exp2(byte - 127.0)
    codes = (blocks / scale).astype(np.float32).astype(dtype).astype(np.float64)
    return np.moveaxis((codes * scale).reshape(v.shape), -1, axis)


WIDE = False


def mx_kscale(k):
    if not WIDE:
        return np.ones(k)
    levels = np.array([10, -10, 5, -5, 0])
    if k % 512:
        return np.exp2(np.random.permutation(np.resize(levels, k // 32))).repeat(32)
    a = np.empty((k // 512, 16))
    for p in range(k // 512):
        a[p, :8] = np.random.permutation(np.resize(levels, 8))
        for g in range(8):
            far = levels[np.abs(levels - a[p, g]) >= 10]
            a[p, g + 8] = far[np.random.randint(len(far))]
    return np.exp2(a.ravel()).repeat(32)


def f64(x):
    return np.asarray(x).astype(np.float64)


def striped(idx):
    return np.tile(np.asarray(idx).reshape(-1, 16).T, (8, 1)).astype(np.uint16)


def unstriped(offs):
    return offs[:16].T.reshape(-1).astype(np.int64)


def striped8(idx):
    return np.asarray(idx).reshape(8, -1, 16).transpose(0, 2, 1).reshape(128, -1).astype(np.uint16)


def unstriped8(offs):
    return offs.reshape(8, 16, -1).transpose(0, 2, 1).reshape(8, -1).astype(np.int64)


def pick8(x, idx, run):
    r = np.arange(len(x))
    return x[r[:, None], idx[r % (8 * run) // run]]


E2M1 = np.array([0.0, 0.5, 1.0, 1.5, 2.0, 3.0, 4.0, 6.0, -0.0, -0.5, -1.0, -1.5, -2.0, -3.0, -4.0, -6.0])


def pack_weight(w, fmt):
    k, n = w.shape
    w = f64(np.asarray(w, np.float32).astype(ml_dtypes.bfloat16)).reshape(k // 32, 32, n)
    amax = np.abs(w).max(1)
    if fmt == "e4m3":
        byte = np.frexp(amax)[1] - 1 + 127 - 7
    else:
        mant, ex = np.frexp(amax / 6.0)
        byte = np.where(mant > 0.5, ex, ex - 1) + 127
    byte = np.clip(np.where(amax > 0, byte, 1), 1, 254)
    scaled = (w * np.exp2(127.0 - byte)[:, None, :]).reshape(k, n).astype(np.float32)
    by_word = np.ascontiguousarray(scaled.reshape(k // 512, 128, 4, n).transpose(0, 1, 3, 2))
    if fmt == "e4m3":
        words = by_word.astype(ml_dtypes.float8_e4m3fn).view(np.uint8)
    else:
        c = by_word.astype(ml_dtypes.float4_e2m1fn).view(np.uint8) & 0xF
        words = (c[..., 0::2] | (c[..., 1::2] << 4)).reshape(k // 512, 128, 2 * n)
    return np.ascontiguousarray(words), np.ascontiguousarray(byte.astype(np.uint8).reshape(k // 512, 16, n))


def unpack_weight(words, scales, fmt):
    g, _, n = scales.shape
    words = np.ascontiguousarray(words).reshape(g, 128, n, -1)
    if fmt == "e4m3":
        vals = words.view(ml_dtypes.float8_e4m3fn).astype(np.float64)
    else:
        nib = np.empty((g, 128, n, 4), np.uint8)
        nib[..., 0::2] = words & 0xF
        nib[..., 1::2] = words >> 4
        vals = E2M1[nib]
    vals = vals * np.repeat(np.exp2(scales.astype(np.float64) - 127.0), 8, axis=1)[..., None]
    return vals.transpose(0, 1, 3, 2).reshape(g * 512, n)


def sgn(shape):
    return np.random.uniform(0.5, 2.0, shape) * np.where(np.random.standard_normal(shape) < 0, -1.0, 1.0)


K, J, R, T, F, O, N, S, U, E = 512, 1024, 512, 4096, 2048, 512, 256, 1024, 256, 1024


def setup_inputs():
    n = np.random.standard_normal
    idx = np.random.permutation(T)[:J]
    idx2 = np.stack([np.random.permutation(F)[:R] for _ in range(8)])
    idx3 = np.random.permutation(J)[:O]
    idx4 = np.stack([np.random.permutation(J)[:O] for _ in range(8)])
    idx5 = np.random.permutation(S)[:N]
    idx6 = np.stack([np.random.permutation(O)[:U] for _ in range(8)])
    idx7 = np.stack([np.random.permutation(E)[:U] for _ in range(8)])
    fk = mx_kscale(K)
    fr = mx_kscale(R)
    xtp = pack_weight(n((K, T)) * fk[:, None], "e4m3")
    vsp = pack_weight(n((R, S)) * 1 / np.sqrt(R) / fr[:, None], "e4m3")
    return {
        "xt_words": xtp[0],
        "xt_scales": xtp[1],
        "ua": (np.random.randint(-7, 8, (K, F)).astype(np.float64)).astype(np.float32),
        "ha": ((np.random.randint(8, 25, (K, 1)) / 1024.0) / fk[:, None]).astype(np.float32),
        "sa": (np.random.uniform(0.5, 1.6, (R, 1)) * fr[:, None]).astype(np.float32),
        "sb": (np.random.uniform(0.5, 1.6, (R, 1)) * fr[:, None]).astype(np.float32),
        "vs_words": vsp[0],
        "vs_scales": vsp[1],
        "so": (sgn((N, 1))).astype(np.float32),
        "offs": striped(idx),
        "offs2": striped8(idx2),
        "offs3": striped(idx3),
        "offs4": striped8(idx4),
        "offs5": striped(idx5),
        "offs6": striped8(idx6),
        "offs7": striped8(idx7),
    }


def reference(xt_words, xt_scales, ua, ha, sa, sb, vs_words, vs_scales, so, offs, offs2, offs3, offs4, offs5, offs6, offs7):
    idx = unstriped(offs)
    idx2 = unstriped8(offs2)
    idx3 = unstriped(offs3)
    idx4 = unstriped8(offs4)
    idx5 = unstriped(offs5)
    idx6 = unstriped8(offs6)
    idx7 = unstriped8(offs7)
    xtu = unpack_weight(xt_words, xt_scales, "e4m3")
    vsu = unpack_weight(vs_words, vs_scales, "e4m3")
    wc = pick8(f64(ua), idx2, 64) * f64(ha)
    wcq = mxq(wc, 0, "e4m3")
    xtidxg = xtu[:, idx]
    a = wcq.T @ xtidxg
    hid = np.maximum(a[:, idx3] * f64(sa), pick8(a, idx4, 64) * f64(sb))
    vsidx5g = vsu[:, idx5]
    hidq = mxq(hid, 0, "e4m3")
    p = vsidx5g.T @ hidq
    m0 = pick8(p, idx6, 16) * f64(so)
    y = np.zeros((N, E))
    y[np.arange(N)[:, None], idx7[np.arange(N) % 128 // 16]] = m0
    return y

@@ -1,0 +1,215 @@
+from contextlib import ExitStack
+
+import concourse.mybir as mybir
+
+K, J, R, T, F, O, N, S, U, E = 512, 1024, 512, 4096, 2048, 512, 256, 1024, 256, 1024
+FLOPS = 2 * K * R * J + 2 * R * N * O
+
+F32 = mybir.dt.float32
+BF16 = mybir.dt.bfloat16
+I32 = mybir.dt.int32
+U32 = mybir.dt.uint32
+U16 = mybir.dt.uint16
+U8 = mybir.dt.uint8
+FP8X4 = mybir.dt.float8_e4m3fn_x4
+COPY = mybir.ActivationFunctionType.Copy
+MAX = mybir.AluOpType.max
+
+P = 128
+PACK = 4
+LANE = 16
+
+
+def entries(offsets, lo, hi):
+    return offsets[:, lo // LANE : hi // LANE]
+
+
+def tile_picked_tokens_codes_one_mixedpair_store_posted_kernel(
+    tc, xt_words, xt_scales, ua, ha, sa, sb, vs_words, vs_scales, so,
+    offs, offs2, offs3, offs4, offs5, offs6, offs7, out,
+):
+    nc = tc.nc
+    with ExitStack() as ctx:
+        lists = ctx.enter_context(tc.tile_pool(name="lists", bufs=1))
+        keep = ctx.enter_context(tc.tile_pool(name="keep", bufs=1))
+        psum = ctx.enter_context(tc.psum_pool(name="psum", bufs=1))
+
+        def load_list(src, name):
+            tile = lists.tile(list(src.shape), U16, name=name)
+            nc.sync.dma_start(tile[:], src)
+            return tile
+
+        def load_factor(src, name):
+            tile = keep.tile([P, PACK], F32, name=name)
+            nc.sync.dma_start(tile[:], src.rearrange("(p t) o -> p (t o)", t=PACK))
+            return tile
+
+        def bank(b, width):
+            return psum.tile([P, width], F32, name=f"bank{b}", tag=f"bank{b}")
+
+        xs_win = keep.tile([P, T], U8, name="xs_win", align_bytes=64)
+        nc.vector.memset(xs_win[:].bitcast(I32), 0)
+        xs_plane = keep.tile([P, J], U8, name="xs_plane", align_bytes=64)
+        nc.vector.memset(xs_plane[:].bitcast(I32), 0)
+        vs_win = keep.tile([P, S], U8, name="vs_win", align_bytes=64)
+        nc.vector.memset(vs_win[:].bitcast(I32), 0)
+
+        ua_rows = ua.rearrange("(p t) f -> p t f", t=PACK)
+        ua_win = [keep.tile([P, F], F32, name=f"ua_win{t}") for t in range(PACK)]
+        nc.sync.dma_start(ua_win[0][:], ua_rows[:, 0, :])
+        nc.sync.dma_start(xs_win[0:P:8, :].bitcast(I32), xt_scales[0].bitcast(I32))
+        l2 = load_list(offs2, "l2")
+        ha_t = load_factor(ha, "ha_t")
+        l1 = load_list(offs, "l1")
+        for t in range(1, PACK):
+            nc.sync.dma_start(ua_win[t][:], ua_rows[:, t, :])
+        xw_win = keep.tile([P, T], U32, name="xw_win", align_bytes=64)
+        nc.sync.dma_start(xw_win[:].bitcast(I32), xt_words[0].rearrange("p n t -> p (n t)").bitcast(I32))
+        l3 = load_list(offs3, "l3")
+        l4 = load_list(offs4, "l4")
+        sa_t = load_factor(sa, "sa_t")
+        sb_t = load_factor(sb, "sb_t")
+        vw_win = keep.tile([P, S], U32, name="vw_win", align_bytes=64)
+        nc.sync.dma_start(vw_win[:].bitcast(I32), vs_words[0].rearrange("p n t -> p (n t)").bitcast(I32))
+        l5 = load_list(offs5, "l5")
+        for q in range(4):
+            nc.sync.dma_start(
+                vs_win[32 * q : 32 * q + 4, :].bitcast(I32), vs_scales[0, 4 * q : 4 * q + 4, :].bitcast(I32)
+            )
+        l6 = load_list(offs6, "l6")
+        l7 = load_list(offs7, "l7")
+        so_t = keep.tile([P, N // P], F32, name="so_t")
+        with nc.allow_non_contiguous_dma(reason="one factor a partition for each tile of output features"):
+            nc.sync.dma_start(so_t[:], so.rearrange("(u p) o -> p (u o)", p=P))
+
+        xs_got = keep.tile([P, J], U8, name="xs_got", align_bytes=64)
+        nc.vector.tensor_copy(xs_got[:], xs_win[:].indirect(l1[:]))
+        for q in range(4):
+            nc.gpsimd.dma_start(
+                xs_plane[32 * q : 32 * q + 4, :].bitcast(I32), xs_got[32 * q : 32 * q + 32 : 8, :].bitcast(I32)
+            )
+        page = [keep.tile([P, E], F32, name=f"page{u}") for u in range(N // P)]
+        for u in range(N // P):
+            nc.vector.memset(page[u][:], 0.0)
+
+        wc_rows = keep.tile([P, PACK, R], BF16, name="wc_rows", align_bytes=64)
+        for t in range(PACK):
+            nc.scalar.activation(wc_rows[:, t, :], ua_win[t][:].indirect(l2[:]), COPY, scale=ha_t[:, t : t + 1])
+        wc_in = keep.tile([P, PACK * R], BF16, name="wc_in", align_bytes=64)
+        nc.vector.tensor_copy(
+            wc_in[:].rearrange("p (s m t) -> p s m t", s=PACK, t=PACK),
+            wc_rows[:].rearrange("p t (m s) -> p s m t", s=PACK),
+        )
+        wc_words = keep.tile([P, R], U32, name="wc_words", align_bytes=64)
+        wc_scales = keep.tile([P, R], U8, name="wc_scales", align_bytes=64)
+        nc.vector.quantize_mx(wc_words[:].bitcast(FP8X4), wc_scales[:], wc_in[:])
+
+        xw_got = keep.tile([P, J], U32, name="xw_got", align_bytes=64)
+        a_win = [keep.tile([P, J], F32, name=f"a_win{s}") for s in range(PACK)]
+
+        def first_product(s, lo, hi, b):
+            acc = bank(b, hi - lo)
+            cols = slice(s * P, (s + 1) * P)
+            nc.tensor.matmul_mx(
+                acc[:], lhsT=wc_words[:, cols].bitcast(FP8X4), lhsT_scale=wc_scales[:, cols],
+                rhs=xw_got[:, lo:hi].bitcast(FP8X4), rhs_scale=xs_plane[:, lo:hi], start=True, stop=True,
+            )
+            return acc
+
+        pieces = [(0, 512), (512, 768), (768, 1024)]
+        for b, (lo, hi) in enumerate(pieces):
+            nc.vector.tensor_copy(xw_got[:, lo:hi], xw_win[:].indirect(entries(l1, lo, hi)))
+            acc = first_product(0, lo, hi, b)
+            nc.scalar.copy(a_win[0][:, lo:hi], acc[:])
+        for h in range(2):
+            acc = first_product(1, 512 * h, 512 * h + 512, 3 + h)
+            nc.vector.tensor_copy(a_win[1][:, 512 * h : 512 * h + 512], acc[:])
+        for s in (2, 3):
+            acc = first_product(s, 0, 512, 3 + s)
+            nc.vector.tensor_copy(a_win[s][:, 0:512], acc[:])
+        late = {2: first_product(2, 512, 1024, 7), 3: first_product(3, 512, 1024, 0)}
+        for h in range(2):
+            for s in (2, 3):
+                nc.vector.tensor_copy(
+                    a_win[s][:, 512 + 256 * h : 768 + 256 * h], late[s][:, 256 * h : 256 * h + 256]
+                )
+
+        vw_got = keep.tile([P, N], U32, name="vw_got", align_bytes=64)
+        nc.vector.tensor_copy(vw_got[:], vw_win[:].indirect(l5[:]))
+        vs_got = keep.tile([P, N], U8, name="vs_got", align_bytes=64)
+        nc.vector.tensor_copy(vs_got[:], vs_win[:].indirect(l5[:]))
+
+        ga = keep.tile([P, PACK, O], F32, name="ga", align_bytes=64)
+        gb = keep.tile([P, PACK, O], F32, name="gb", align_bytes=64)
+
+        def fetch_a(s, lo, hi):
+            nc.scalar.activation(
+                ga[:, s, lo:hi], a_win[s][:].indirect(entries(l3, lo, hi)), COPY, scale=sa_t[:, s : s + 1]
+            )
+
+        def fetch_b(s, lo, hi):
+            nc.scalar.activation(
+                gb[:, s, lo:hi], a_win[s][:].indirect(entries(l4, lo, hi)), COPY, scale=sb_t[:, s : s + 1]
+            )
+
+        def larger(lo, hi):
+            hid = keep.tile([P, PACK * (hi - lo)], BF16, name=f"hid{lo}", align_bytes=64)
+            nc.vector.tensor_tensor(
+                hid[:].rearrange("p (c i t) -> p c t i", i=4, t=PACK),
+                ga[:, :, lo:hi].rearrange("p t (c i) -> p c t i", i=4),
+                gb[:, :, lo:hi].rearrange("p t (c i) -> p c t i", i=4),
+                MAX,
+            )
+            return hid
+
+        def quantise(hid, lo, hi):
+            words = keep.tile([P, hi - lo], U32, name=f"hid_words{lo}", align_bytes=64)
+            scales = keep.tile([P, hi - lo], U8, name=f"hid_scales{lo}", align_bytes=64)
+            nc.vector.quantize_mx(words[:].bitcast(FP8X4), scales[:], hid[:])
+            return words, scales
+
+        def second_product(u, acc, words, scales):
+            cols = slice(u * P, (u + 1) * P)
+            nc.tensor.matmul_mx(
+                acc, lhsT=vw_got[:, cols].bitcast(FP8X4), lhsT_scale=vs_got[:, cols],
+                rhs=words[:].bitcast(FP8X4), rhs_scale=scales[:], start=True, stop=True,
+            )
+
+        for s in (0, 1):
+            fetch_b(s, 0, O)
+            fetch_a(s, 0, O)
+        for s in (2, 3):
+            fetch_b(s, 0, 256)
+            fetch_a(s, 0, 256)
+        hid_a = larger(0, 256)
+        q_a = quantise(hid_a, 0, 256)
+        acc_a = [bank(1 + u, 256) for u in range(2)]
+        for u in range(2):
+            second_product(u, acc_a[u][:], *q_a)
+        for s in (2, 3):
+            fetch_b(s, 256, 512)
+        hid_b = []
+        for lo in (256, 384):
+            for s in (2, 3):
+                fetch_a(s, lo, lo + 128)
+            hid_b.append(larger(lo, lo + 128))
+        p_win = [keep.tile([P, O], F32, name=f"p_win{u}") for u in range(N // P)]
+        for u in range(2):
+            nc.scalar.copy(p_win[u][:, 0:256], acc_a[u][:])
+        acc_b = [bank(3 + u, 256) for u in range(2)]
+        for i, lo in enumerate((256, 384)):
+            q_b = quantise(hid_b[i], lo, lo + 128)
+            for u in range(2):
+                second_product(u, acc_b[u][:, 128 * i : 128 * i + 128], *q_b)
+        nc.scalar.copy(p_win[0][:, 256:512], acc_b[0][:])
+        nc.vector.tensor_copy(p_win[1][:, 256:512], acc_b[1][:])
+
+        m0 = [keep.tile([P, U], F32, name=f"m0_{u}") for u in range(N // P)]
+        cuts = [[(0, 128), (128, 256)], [(0, 256)]]
+        for u in range(N // P):
+            for lo, hi in cuts[u]:
+                nc.scalar.activation(
+                    m0[u][:, lo:hi], p_win[u][:].indirect(entries(l6, lo, hi)), COPY, scale=so_t[:, u : u + 1]
+                )
+                nc.vector.tensor_copy(page[u][:].indirect(entries(l7, lo, hi)), m0[u][:, lo:hi])
+            nc.sync.dma_start(out[u * P : (u + 1) * P, :], page[u][:])

@@ -92,14 +92,12 @@ def tile_picked_tokens_codes_one_mixedpair_store_posted_kernel(
         for u in range(N // P):
             nc.vector.memset(page[u][:], 0.0)
 
-        wc_rows = keep.tile([P, PACK, R], BF16, name="wc_rows", align_bytes=64)
-        for t in range(PACK):
-            nc.scalar.activation(wc_rows[:, t, :], ua_win[t][:].indirect(l2[:]), COPY, scale=ha_t[:, t : t + 1])
         wc_in = keep.tile([P, PACK * R], BF16, name="wc_in", align_bytes=64)
-        nc.vector.tensor_copy(
-            wc_in[:].rearrange("p (s m t) -> p s m t", s=PACK, t=PACK),
-            wc_rows[:].rearrange("p t (m s) -> p s m t", s=PACK),
-        )
+        wc_dealt = wc_in[:].rearrange("p (s m t) -> p t m s", s=PACK, t=PACK)
+        for t in range(PACK):
+            wc_row = keep.tile([P, R], BF16, name=f"wc_row{t}", align_bytes=64)
+            nc.scalar.activation(wc_row[:], ua_win[t][:].indirect(l2[:]), COPY, scale=ha_t[:, t : t + 1])
+            nc.vector.tensor_copy(wc_dealt[:, t], wc_row[:].rearrange("p (m s) -> p m s", s=PACK))
         wc_words = keep.tile([P, R], U32, name="wc_words", align_bytes=64)
         wc_scales = keep.tile([P, R], U8, name="wc_scales", align_bytes=64)
         nc.vector.quantize_mx(wc_words[:].bitcast(FP8X4), wc_scales[:], wc_in[:])
@@ -116,11 +114,15 @@ def tile_picked_tokens_codes_one_mixedpair_store_posted_kernel(
             )
             return acc
 
-        pieces = [(0, 512), (512, 768), (768, 1024)]
-        for b, (lo, hi) in enumerate(pieces):
+        for b, (lo, hi) in enumerate([(0, 512), (512, 768)]):
             nc.vector.tensor_copy(xw_got[:, lo:hi], xw_win[:].indirect(entries(l1, lo, hi)))
             acc = first_product(0, lo, hi, b)
             nc.scalar.copy(a_win[0][:, lo:hi], acc[:])
+        nc.vector.tensor_copy(xw_got[:, 768:1024], xw_win[:].indirect(entries(l1, 768, 1024)))
+        acc = first_product(0, 768, 896, 2)
+        nc.scalar.copy(a_win[0][:, 768:896], acc[:])
+        acc = first_product(0, 896, 1024, 7)
+        nc.vector.tensor_copy(a_win[0][:, 896:1024], acc[:])
         for h in range(2):
             acc = first_product(1, 512 * h, 512 * h + 512, 3 + h)
             nc.vector.tensor_copy(a_win[1][:, 512 * h : 512 * h + 512], acc[:])
@@ -196,13 +198,16 @@ def tile_picked_tokens_codes_one_mixedpair_store_posted_kernel(
         p_win = [keep.tile([P, O], F32, name=f"p_win{u}") for u in range(N // P)]
         for u in range(2):
             nc.scalar.copy(p_win[u][:, 0:256], acc_a[u][:])
-        acc_b = [bank(3 + u, 256) for u in range(2)]
-        for i, lo in enumerate((256, 384)):
-            q_b = quantise(hid_b[i], lo, lo + 128)
-            for u in range(2):
-                second_product(u, acc_b[u][:, 128 * i : 128 * i + 128], *q_b)
-        nc.scalar.copy(p_win[0][:, 256:512], acc_b[0][:])
-        nc.vector.tensor_copy(p_win[1][:, 256:512], acc_b[1][:])
+        q_b1 = quantise(hid_b[0], 256, 384)
+        q_b2 = quantise(hid_b[1], 384, 512)
+        acc_b1, acc_b2, acc_b = bank(3, 128), bank(4, 128), bank(5, 256)
+        second_product(0, acc_b1[:], *q_b1)
+        nc.scalar.copy(p_win[0][:, 256:384], acc_b1[:])
+        second_product(1, acc_b[:, 0:128], *q_b1)
+        second_product(0, acc_b2[:], *q_b2)
+        nc.scalar.copy(p_win[0][:, 384:512], acc_b2[:])
+        second_product(1, acc_b[:, 128:256], *q_b2)
+        nc.vector.tensor_copy(p_win[1][:, 256:512], acc_b[:])
 
         m0 = [keep.tile([P, U], F32, name=f"m0_{u}") for u in range(N // P)]
         cuts = [[(0, 128), (128, 256)], [(0, 256)]]

from contextlib import ExitStack

import concourse.mybir as mybir

K, J, R, T, F, O, N, S, U, E = 512, 1024, 512, 4096, 2048, 512, 256, 1024, 256, 1024
FLOPS = 2 * K * R * J + 2 * R * N * O

F32 = mybir.dt.float32
BF16 = mybir.dt.bfloat16
I32 = mybir.dt.int32
U32 = mybir.dt.uint32
U16 = mybir.dt.uint16
U8 = mybir.dt.uint8
FP8X4 = mybir.dt.float8_e4m3fn_x4
COPY = mybir.ActivationFunctionType.Copy
MAX = mybir.AluOpType.max

P = 128
PACK = 4
LANE = 16


def entries(offsets, lo, hi):
    return offsets[:, lo // LANE : hi // LANE]


def tile_picked_tokens_codes_one_mixedpair_store_posted_kernel(
    tc, xt_words, xt_scales, ua, ha, sa, sb, vs_words, vs_scales, so,
    offs, offs2, offs3, offs4, offs5, offs6, offs7, out,
):
    nc = tc.nc
    with ExitStack() as ctx:
        lists = ctx.enter_context(tc.tile_pool(name="lists", bufs=1))
        keep = ctx.enter_context(tc.tile_pool(name="keep", bufs=1))
        psum = ctx.enter_context(tc.psum_pool(name="psum", bufs=1))

        def load_list(src, name):
            tile = lists.tile(list(src.shape), U16, name=name)
            nc.sync.dma_start(tile[:], src)
            return tile

        def load_factor(src, name):
            tile = keep.tile([P, PACK], F32, name=name)
            nc.sync.dma_start(tile[:], src.rearrange("(p t) o -> p (t o)", t=PACK))
            return tile

        def bank(b, width):
            return psum.tile([P, width], F32, name=f"bank{b}", tag=f"bank{b}")

        xs_win = keep.tile([P, T], U8, name="xs_win", align_bytes=64)
        nc.vector.memset(xs_win[:].bitcast(I32), 0)
        xs_plane = keep.tile([P, J], U8, name="xs_plane", align_bytes=64)
        nc.vector.memset(xs_plane[:].bitcast(I32), 0)
        vs_win = keep.tile([P, S], U8, name="vs_win", align_bytes=64)
        nc.vector.memset(vs_win[:].bitcast(I32), 0)

        ua_rows = ua.rearrange("(p t) f -> p t f", t=PACK)
        ua_win = [keep.tile([P, F], F32, name=f"ua_win{t}") for t in range(PACK)]
        nc.sync.dma_start(ua_win[0][:], ua_rows[:, 0, :])
        nc.sync.dma_start(xs_win[0:P:8, :].bitcast(I32), xt_scales[0].bitcast(I32))
        l2 = load_list(offs2, "l2")
        ha_t = load_factor(ha, "ha_t")
        l1 = load_list(offs, "l1")
        for t in range(1, PACK):
            nc.sync.dma_start(ua_win[t][:], ua_rows[:, t, :])
        xw_win = keep.tile([P, T], U32, name="xw_win", align_bytes=64)
        nc.sync.dma_start(xw_win[:].bitcast(I32), xt_words[0].rearrange("p n t -> p (n t)").bitcast(I32))
        l3 = load_list(offs3, "l3")
        l4 = load_list(offs4, "l4")
        sa_t = load_factor(sa, "sa_t")
        sb_t = load_factor(sb, "sb_t")
        vw_win = keep.tile([P, S], U32, name="vw_win", align_bytes=64)
        nc.sync.dma_start(vw_win[:].bitcast(I32), vs_words[0].rearrange("p n t -> p (n t)").bitcast(I32))
        l5 = load_list(offs5, "l5")
        for q in range(4):
            nc.sync.dma_start(
                vs_win[32 * q : 32 * q + 4, :].bitcast(I32), vs_scales[0, 4 * q : 4 * q + 4, :].bitcast(I32)
            )
        l6 = load_list(offs6, "l6")
        l7 = load_list(offs7, "l7")
        so_t = keep.tile([P, N // P], F32, name="so_t")
        with nc.allow_non_contiguous_dma(reason="one factor a partition for each tile of output features"):
            nc.sync.dma_start(so_t[:], so.rearrange("(u p) o -> p (u o)", p=P))

        xs_got = keep.tile([P, J], U8, name="xs_got", align_bytes=64)
        nc.vector.tensor_copy(xs_got[:], xs_win[:].indirect(l1[:]))
        for q in range(4):
            nc.gpsimd.dma_start(
                xs_plane[32 * q : 32 * q + 4, :].bitcast(I32), xs_got[32 * q : 32 * q + 32 : 8, :].bitcast(I32)
            )
        page = [keep.tile([P, E], F32, name=f"page{u}") for u in range(N // P)]
        for u in range(N // P):
            nc.vector.memset(page[u][:], 0.0)

        wc_in = keep.tile([P, PACK * R], BF16, name="wc_in", align_bytes=64)
        wc_dealt = wc_in[:].rearrange("p (s m t) -> p t m s", s=PACK, t=PACK)
        for t in range(PACK):
            wc_row = keep.tile([P, R], BF16, name=f"wc_row{t}", align_bytes=64)
            nc.scalar.activation(wc_row[:], ua_win[t][:].indirect(l2[:]), COPY, scale=ha_t[:, t : t + 1])
            nc.vector.tensor_copy(wc_dealt[:, t], wc_row[:].rearrange("p (m s) -> p m s", s=PACK))
        wc_words = keep.tile([P, R], U32, name="wc_words", align_bytes=64)
        wc_scales = keep.tile([P, R], U8, name="wc_scales", align_bytes=64)
        nc.vector.quantize_mx(wc_words[:].bitcast(FP8X4), wc_scales[:], wc_in[:])

        xw_got = keep.tile([P, J], U32, name="xw_got", align_bytes=64)
        a_win = [keep.tile([P, J], F32, name=f"a_win{s}") for s in range(PACK)]

        def first_product(s, lo, hi, b):
            acc = bank(b, hi - lo)
            cols = slice(s * P, (s + 1) * P)
            nc.tensor.matmul_mx(
                acc[:], lhsT=wc_words[:, cols].bitcast(FP8X4), lhsT_scale=wc_scales[:, cols],
                rhs=xw_got[:, lo:hi].bitcast(FP8X4), rhs_scale=xs_plane[:, lo:hi], start=True, stop=True,
            )
            return acc

        for b, (lo, hi) in enumerate([(0, 512), (512, 768)]):
            nc.vector.tensor_copy(xw_got[:, lo:hi], xw_win[:].indirect(entries(l1, lo, hi)))
            acc = first_product(0, lo, hi, b)
            nc.scalar.copy(a_win[0][:, lo:hi], acc[:])
        nc.vector.tensor_copy(xw_got[:, 768:1024], xw_win[:].indirect(entries(l1, 768, 1024)))
        acc = first_product(0, 768, 896, 2)
        nc.scalar.copy(a_win[0][:, 768:896], acc[:])
        acc = first_product(0, 896, 1024, 7)
        nc.vector.tensor_copy(a_win[0][:, 896:1024], acc[:])
        for h in range(2):
            acc = first_product(1, 512 * h, 512 * h + 512, 3 + h)
            nc.vector.tensor_copy(a_win[1][:, 512 * h : 512 * h + 512], acc[:])
        for s in (2, 3):
            acc = first_product(s, 0, 512, 3 + s)
            nc.vector.tensor_copy(a_win[s][:, 0:512], acc[:])
        late = {2: first_product(2, 512, 1024, 7), 3: first_product(3, 512, 1024, 0)}
        for h in range(2):
            for s in (2, 3):
                nc.vector.tensor_copy(
                    a_win[s][:, 512 + 256 * h : 768 + 256 * h], late[s][:, 256 * h : 256 * h + 256]
                )

        vw_got = keep.tile([P, N], U32, name="vw_got", align_bytes=64)
        nc.vector.tensor_copy(vw_got[:], vw_win[:].indirect(l5[:]))
        vs_got = keep.tile([P, N], U8, name="vs_got", align_bytes=64)
        nc.vector.tensor_copy(vs_got[:], vs_win[:].indirect(l5[:]))

        ga = keep.tile([P, PACK, O], F32, name="ga", align_bytes=64)
        gb = keep.tile([P, PACK, O], F32, name="gb", align_bytes=64)

        def fetch_a(s, lo, hi):
            nc.scalar.activation(
                ga[:, s, lo:hi], a_win[s][:].indirect(entries(l3, lo, hi)), COPY, scale=sa_t[:, s : s + 1]
            )

        def fetch_b(s, lo, hi):
            nc.scalar.activation(
                gb[:, s, lo:hi], a_win[s][:].indirect(entries(l4, lo, hi)), COPY, scale=sb_t[:, s : s + 1]
            )

        def larger(lo, hi):
            hid = keep.tile([P, PACK * (hi - lo)], BF16, name=f"hid{lo}", align_bytes=64)
            nc.vector.tensor_tensor(
                hid[:].rearrange("p (c i t) -> p c t i", i=4, t=PACK),
                ga[:, :, lo:hi].rearrange("p t (c i) -> p c t i", i=4),
                gb[:, :, lo:hi].rearrange("p t (c i) -> p c t i", i=4),
                MAX,
            )
            return hid

        def quantise(hid, lo, hi):
            words = keep.tile([P, hi - lo], U32, name=f"hid_words{lo}", align_bytes=64)
            scales = keep.tile([P, hi - lo], U8, name=f"hid_scales{lo}", align_bytes=64)
            nc.vector.quantize_mx(words[:].bitcast(FP8X4), scales[:], hid[:])
            return words, scales

        def second_product(u, acc, words, scales):
            cols = slice(u * P, (u + 1) * P)
            nc.tensor.matmul_mx(
                acc, lhsT=vw_got[:, cols].bitcast(FP8X4), lhsT_scale=vs_got[:, cols],
                rhs=words[:].bitcast(FP8X4), rhs_scale=scales[:], start=True, stop=True,
            )

        for s in (0, 1):
            fetch_b(s, 0, O)
            fetch_a(s, 0, O)
        for s in (2, 3):
            fetch_b(s, 0, 256)
            fetch_a(s, 0, 256)
        hid_a = larger(0, 256)
        q_a = quantise(hid_a, 0, 256)
        acc_a = [bank(1 + u, 256) for u in range(2)]
        for u in range(2):
            second_product(u, acc_a[u][:], *q_a)
        for s in (2, 3):
            fetch_b(s, 256, 512)
        hid_b = []
        for lo in (256, 384):
            for s in (2, 3):
                fetch_a(s, lo, lo + 128)
            hid_b.append(larger(lo, lo + 128))
        p_win = [keep.tile([P, O], F32, name=f"p_win{u}") for u in range(N // P)]
        for u in range(2):
            nc.scalar.copy(p_win[u][:, 0:256], acc_a[u][:])
        q_b1 = quantise(hid_b[0], 256, 384)
        q_b2 = quantise(hid_b[1], 384, 512)
        acc_b1, acc_b2, acc_b = bank(3, 128), bank(4, 128), bank(5, 256)
        second_product(0, acc_b1[:], *q_b1)
        nc.scalar.copy(p_win[0][:, 256:384], acc_b1[:])
        second_product(1, acc_b[:, 0:128], *q_b1)
        second_product(0, acc_b2[:], *q_b2)
        nc.scalar.copy(p_win[0][:, 384:512], acc_b2[:])
        second_product(1, acc_b[:, 128:256], *q_b2)
        nc.vector.tensor_copy(p_win[1][:, 256:512], acc_b[:])

        m0 = [keep.tile([P, U], F32, name=f"m0_{u}") for u in range(N // P)]
        cuts = [[(0, 128), (128, 256)], [(0, 256)]]
        for u in range(N // P):
            for lo, hi in cuts[u]:
                nc.scalar.activation(
                    m0[u][:, lo:hi], p_win[u][:].indirect(entries(l6, lo, hi)), COPY, scale=so_t[:, u : u + 1]
                )
                nc.vector.tensor_copy(page[u][:].indirect(entries(l7, lo, hi)), m0[u][:, lo:hi])
            nc.sync.dma_start(out[u * P : (u + 1) * P, :], page[u][:])
